import numpy as np
import ml_dtypes


def mxq(x, axis, fmt="e4m3"):
    dtype, down = {"e4m3": (ml_dtypes.float8_e4m3fn, 7), "e5m2": (ml_dtypes.float8_e5m2, 14)}[fmt]
    v = np.moveaxis(np.asarray(x, np.float32).astype(ml_dtypes.bfloat16).astype(np.float64), axis, -1)
    blocks = v.reshape(v.shape[:-1] + (-1, 32))
    amax = np.abs(blocks).max(-1, keepdims=True)
    byte = np.maximum(np.where(amax > 0, np.frexp(amax)[1] - 1 + 127, 0) - down, 1)
    scale = np.exp2(byte - 127.0)
    codes = (blocks / scale).astype(np.float32).astype(dtype).astype(np.float64)
    return np.moveaxis((codes * scale).reshape(v.shape), -1, axis)


WIDE = False


def mx_kscale(k):
    if not WIDE:
        return np.ones(k)
    levels = np.array([10, -10, 5, -5, 0])
    if k % 512:
        return np.exp2(np.random.permutation(np.resize(levels, k // 32))).repeat(32)
    a = np.empty((k // 512, 16))
    for p in range(k // 512):
        a[p, :8] = np.random.permutation(np.resize(levels, 8))
        for g in range(8):
            far = levels[np.abs(levels - a[p, g]) >= 10]
            a[p, g + 8] = far[np.random.randint(len(far))]
    return np.exp2(a.ravel()).repeat(32)


def f64(x):
    return np.asarray(x).astype(np.float64)


def striped(idx):
    return np.tile(np.asarray(idx).reshape(-1, 16).T, (8, 1)).astype(np.uint16)


def unstriped(offs):
    return offs[:16].T.reshape(-1).astype(np.int64)


E2M1 = np.array([0.0, 0.5, 1.0, 1.5, 2.0, 3.0, 4.0, 6.0, -0.0, -0.5, -1.0, -1.5, -2.0, -3.0, -4.0, -6.0])


def pack_weight(w, fmt):
    k, n = w.shape
    w = f64(np.asarray(w, np.float32).astype(ml_dtypes.bfloat16)).reshape(k // 32, 32, n)
    amax = np.abs(w).max(1)
    if fmt == "e4m3":
        byte = np.frexp(amax)[1] - 1 + 127 - 7
    else:
        mant, ex = np.frexp(amax / 6.0)
        byte = np.where(mant > 0.5, ex, ex - 1) + 127
    byte = np.clip(np.where(amax > 0, byte, 1), 1, 254)
    scaled = (w * np.exp2(127.0 - byte)[:, None, :]).reshape(k, n).astype(np.float32)
    by_word = np.ascontiguousarray(scaled.reshape(k // 512, 128, 4, n).transpose(0, 1, 3, 2))
    if fmt == "e4m3":
        words = by_word.astype(ml_dtypes.float8_e4m3fn).view(np.uint8)
    else:
        c = by_word.astype(ml_dtypes.float4_e2m1fn).view(np.uint8) & 0xF
        words = (c[..., 0::2] | (c[..., 1::2] << 4)).reshape(k // 512, 128, 2 * n)
    return np.ascontiguousarray(words), np.ascontiguousarray(byte.astype(np.uint8).reshape(k // 512, 16, n))


def unpack_weight(words, scales, fmt):
    g, _, n = scales.shape
    words = np.ascontiguousarray(words).reshape(g, 128, n, -1)
    if fmt == "e4m3":
        vals = words.view(ml_dtypes.float8_e4m3fn).astype(np.float64)
    else:
        nib = np.empty((g, 128, n, 4), np.uint8)
        nib[..., 0::2] = words & 0xF
        nib[..., 1::2] = words >> 4
        vals = E2M1[nib]
    vals = vals * np.repeat(np.exp2(scales.astype(np.float64) - 127.0), 8, axis=1)[..., None]
    return vals.transpose(0, 1, 3, 2).reshape(g * 512, n)


def bf(x):
    return np.asarray(x, np.float32).astype(ml_dtypes.bfloat16)


def planes(Y):
    r, m = Y.shape
    b = f64(bf(Y)).reshape(r // 32, 32, m)
    amax = np.abs(b).max(1)
    byte = np.clip(np.where(amax > 0, np.frexp(amax)[1] - 1 + 127 - 7, 1), 1, 254)
    codes = (b * np.exp2(127.0 - byte)[:, None, :]).reshape(r, m).astype(np.float32).astype(ml_dtypes.float8_e4m3fn).view(np.uint8)
    words = codes.reshape(r // 512, 128, 4, m).transpose(0, 1, 3, 2)
    return np.ascontiguousarray(words), np.ascontiguousarray(byte.astype(np.uint8).reshape(r // 512, 16, m))


D, E, T, I, U, Q = 512, 512, 2048, 256, 1024, 512


def setup_inputs():
    n = np.random.standard_normal
    idx = np.random.permutation(T)[:I]
    idx2 = np.random.permutation(U)[:I]
    fd = mx_kscale(D)
    fq = mx_kscale(Q)
    keysp = pack_weight(n((D, T)) / fd[:, None], "e4m3")
    return {
        "query": (n((D, Q)) * 0.5 / np.sqrt(D) * fd[:, None]).astype(np.float32),
        "keys_words": keysp[0],
        "keys_scales": keysp[1],
        "qs": (np.random.uniform(8.0, 32.0, (Q, 1)) * fq[:, None]).astype(np.float32),
        "grows": (n((Q, E)) / fq[:, None]).astype(np.float32),
        "old": (n((E, U)) * 4.0).astype(np.float32),
        "fade": (np.random.uniform(0.5, 1.0, (1, U))).astype(np.float32),
        "offs": striped(idx),
        "offs2": striped(idx2),
    }


def reference(query, keys_words, keys_scales, qs, grows, old, fade, offs, offs2):
    idx = unstriped(offs)
    idx2 = unstriped(offs2)
    keysu = unpack_weight(keys_words, keys_scales, "e4m3")
    queryq = mxq(f64(query), 0, "e4m3")
    keysidxg = keysu[:, idx]
    a = queryq.T @ keysidxg
    p = np.exp(a - np.max(a, axis=1, keepdims=True))
    w = p * f64(qs) / np.sum(p, axis=1, keepdims=True)
    growsq = mxq(f64(grows), 0, "e4m3")
    wq = mxq(w, 0, "e4m3")
    dv = growsq.T @ wq
    vf = np.zeros((E, U))
    vf[:, idx2] = dv
    y = f64(old) * f64(fade) + vf
    words, scales = planes(y)
    return y, words, scales

@@ -1,0 +1,216 @@
+from contextlib import ExitStack
+
+import concourse.mybir as mybir
+from concourse.masks import make_identity
+
+D, E, T, I, U, Q = 512, 512, 2048, 256, 1024, 512
+FLOPS = 2 * D * Q * I + 2 * Q * E * I
+
+F32 = mybir.dt.float32
+BF16 = mybir.dt.bfloat16
+I32 = mybir.dt.int32
+U32 = mybir.dt.uint32
+U16 = mybir.dt.uint16
+U8 = mybir.dt.uint8
+FP8X4 = mybir.dt.float8_e4m3fn_x4
+ALU = mybir.AluOpType
+ACT = mybir.ActivationFunctionType
+AXIS = mybir.AxisListType
+
+P = 128
+PACK = 4
+HALF = I // 2
+CHUNK = 256
+CHUNKS = U // CHUNK
+BLOCKS = U // P
+
+
+def tile_attend_gvaluestore_pl_kernel(tc, query, keys_words, keys_scales, qs, grows, old, fade, offs, offs2, out_0, out_1, out_2):
+    nc = tc.nc
+    with ExitStack() as ctx:
+        sb = ctx.enter_context(tc.tile_pool(name="sb", bufs=1))
+        ps = ctx.enter_context(tc.psum_pool(name="ps", bufs=1))
+
+        def bank(number, shape, name):
+            return ps.tile(shape, F32, name=name, tag="bank%d" % number)
+
+        key_list = sb.tile([P, I // 16], U16, name="key_list")
+        place_list = sb.tile([P, I // 16], U16, name="place_list")
+        key_words = sb.tile([P, T], I32, name="key_words")
+        key_bytes = sb.tile([P, T], U8, name="key_bytes")
+        fade_rows = sb.tile([P, P], F32, name="fade_rows")
+        identity = sb.tile([P, P], F32, name="identity")
+        row_scale = sb.tile([P, PACK], F32, name="row_scale")
+        query_raw = [sb.tile([P, PACK, Q // 2], F32, name="query_raw%d" % h) for h in range(2)]
+        grows_raw = [sb.tile([P, PACK, E // 2], F32, name="grows_raw%d" % h) for h in range(2)]
+        old_raw = [sb.tile([P, PACK, CHUNK], F32, name="old_raw%d" % c) for c in range(CHUNKS)]
+        placed = [sb.tile([P, U], F32, name="placed%d" % j) for j in range(PACK)]
+
+        nc.vector.memset(key_bytes[:].bitcast(I32), 0)
+        nc.gpsimd.memset(fade_rows[:], 0.0)
+        make_identity(nc, identity[:])
+
+        query_rows = query.rearrange("(p t) q -> p t q", t=PACK)
+        grows_rows = grows.rearrange("(p t) e -> p t e", t=PACK)
+        old_rows = old.rearrange("(p j) u -> p j u", j=PACK)
+        out_rows = out_0.rearrange("(p j) u -> p j u", j=PACK)
+
+        nc.sync.dma_start(key_list[:], offs)
+        for h in range(2):
+            nc.sync.dma_start(query_raw[h][:], query_rows[:, :, h * (Q // 2) : (h + 1) * (Q // 2)])
+        for quad in range(4):
+            nc.scalar.dma_start(
+                key_bytes[32 * quad : 32 * quad + 4, :].bitcast(I32),
+                keys_scales[0, 4 * quad : 4 * quad + 4, :].bitcast(I32),
+            )
+        nc.sync.dma_start(key_words[:], keys_words[0].rearrange("p c r -> p (c r)").bitcast(I32))
+        for h in range(2):
+            nc.sync.dma_start(grows_raw[h][:], grows_rows[:, :, h * (E // 2) : (h + 1) * (E // 2)])
+        nc.sync.dma_start(row_scale[:], qs.rearrange("(p r) o -> p (r o)", r=PACK))
+        nc.sync.dma_start(fade_rows[0:BLOCKS, :], fade.rearrange("o (b p) -> (o b) p", p=P))
+        nc.sync.dma_start(place_list[:], offs2)
+        for c in range(CHUNKS):
+            nc.sync.dma_start(old_raw[c][:], old_rows[:, :, c * CHUNK : (c + 1) * CHUNK])
+
+        for j in range(PACK):
+            nc.vector.memset(placed[j][:], 0.0)
+
+        def deal(copy, dealt, raw, h):
+            copy(
+                dealt[:, :, 64 * h : 64 * (h + 1), :].rearrange("p r s t -> p s t r"),
+                raw[:].rearrange("p t (s r) -> p s t r", r=PACK),
+            )
+
+        query_dealt = sb.tile([P, PACK, P, PACK], BF16, name="query_dealt", align_bytes=64)
+        query_codes = sb.tile([P, Q], U32, name="query_codes", align_bytes=64)
+        query_bytes = sb.tile([P, Q], U8, name="query_bytes", align_bytes=64)
+        for h in range(2):
+            deal(nc.vector.tensor_copy, query_dealt, query_raw[h], h)
+        listed_words = sb.tile([P, I], U32, name="listed_words", align_bytes=64)
+        listed_bytes = sb.tile([P, I], U8, name="listed_bytes", align_bytes=64)
+        nc.vector.tensor_copy(listed_bytes[:], key_bytes[:].indirect(key_list[:]))
+        nc.vector.quantize_mx(query_codes[:].bitcast(FP8X4), query_bytes[:], query_dealt[:].rearrange("p r s t -> p (r s t)"))
+        nc.vector.tensor_copy(listed_words[:], key_words[:].bitcast(U32).indirect(key_list[:]))
+
+        weights = sb.tile([P, PACK, I], F32, name="weights")
+        neg_max = sb.tile([P, PACK], F32, name="neg_max")
+        row_sum = sb.tile([P, PACK], F32, name="row_sum")
+        for r in range(PACK):
+            scores = bank(r, [P, I], "scores%d" % r)
+            nc.tensor.matmul_mx(
+                scores[:],
+                lhsT=query_codes[:, r * P : (r + 1) * P].bitcast(FP8X4),
+                lhsT_scale=query_bytes[:, r * P : (r + 1) * P],
+                rhs=listed_words[:].bitcast(FP8X4),
+                rhs_scale=listed_bytes[:],
+                start=True,
+                stop=True,
+            )
+            nc.vector.tensor_reduce(neg_max[:, r : r + 1], scores[:], AXIS.X, ALU.max, negate=True)
+            nc.scalar.activation(weights[:, r, :], scores[:], ACT.Exp, bias=neg_max[:, r : r + 1], accum_out=row_sum[:, r : r + 1])
+
+        grows_dealt = sb.tile([P, PACK, P, PACK], BF16, name="grows_dealt", align_bytes=64)
+        grows_codes = sb.tile([P, E], U32, name="grows_codes", align_bytes=64)
+        grows_bytes = sb.tile([P, E], U8, name="grows_bytes", align_bytes=64)
+        deal(nc.vector.tensor_copy, grows_dealt, grows_raw[0], 0)
+        deal(nc.scalar.copy, grows_dealt, grows_raw[1], 1)
+
+        inv_sum = sb.tile([P, PACK], F32, name="inv_sum")
+        factor = sb.tile([P, PACK], F32, name="factor")
+        nc.vector.reciprocal(inv_sum[:], row_sum[:])
+        nc.vector.tensor_tensor(factor[:], inv_sum[:], row_scale[:], ALU.mult)
+
+        w_bf = [sb.tile([P, HALF, PACK], BF16, name="w_bf%d" % h, align_bytes=64) for h in range(2)]
+        w_codes = [sb.tile([P, HALF], U32, name="w_codes%d" % h, align_bytes=64) for h in range(2)]
+        w_bytes = [sb.tile([P, HALF], U8, name="w_bytes%d" % h, align_bytes=64) for h in range(2)]
+        dv = [sb.tile([P, PACK, HALF], F32, name="dv%d" % h) for h in range(2)]
+
+        def weigh(h):
+            nc.vector.tensor_tensor(
+                w_bf[h][:].rearrange("p (c i) r -> p c r i", i=4),
+                weights[:, :, h * HALF : (h + 1) * HALF].rearrange("p r (c i) -> p c r i", i=4),
+                factor[:].unsqueeze(1).unsqueeze(3).broadcast_to([P, HALF // 4, PACK, 4]),
+                ALU.mult,
+            )
+
+        def quantise_weights(h):
+            nc.vector.quantize_mx(w_codes[h][:].bitcast(FP8X4), w_bytes[h][:], w_bf[h][:].rearrange("p i r -> p (i r)"))
+
+        def value_product(out, h, j):
+            nc.tensor.matmul_mx(
+                out,
+                lhsT=grows_codes[:, j * P : (j + 1) * P].bitcast(FP8X4),
+                lhsT_scale=grows_bytes[:, j * P : (j + 1) * P],
+                rhs=w_codes[h][:].bitcast(FP8X4),
+                rhs_scale=w_bytes[h][:],
+                start=True,
+                stop=True,
+            )
+
+        weigh(0)
+        nc.vector.quantize_mx(grows_codes[:].bitcast(FP8X4), grows_bytes[:], grows_dealt[:].rearrange("p r s t -> p (r s t)"))
+        quantise_weights(0)
+        weigh(1)
+        for j in range(PACK):
+            sums = bank(j, [P, HALF], "dv_first%d" % j)
+            value_product(sums[:], 0, j)
+            nc.scalar.copy(dv[0][:, j, :], sums[:])
+        quantise_weights(1)
+        for pair in range(2):
+            sums = bank(6 + pair, [P, 2, HALF], "dv_second%d" % pair)
+            for k in range(2):
+                value_product(sums[:, k, :], 1, 2 * pair + k)
+            nc.scalar.copy(dv[1][:, 2 * pair : 2 * pair + 2, :], sums[:])
+        for h in range(2):
+            for j in range(PACK):
+                nc.vector.tensor_copy(placed[j][:].indirect(place_list[:, 8 * h : 8 * (h + 1)]), dv[h][:, j, :])
+
+        fade_cols = sb.tile([P, BLOCKS], F32, name="fade_cols")
+        turned_fade = bank(4, [P, P], "turned_fade")
+        nc.tensor.transpose(turned_fade[:], fade_rows[:], identity[:])
+        nc.scalar.copy(fade_cols[:], turned_fade[:, 0:BLOCKS])
+
+        faded = [sb.tile([P, PACK, P], F32, name="faded%d" % b) for b in range(BLOCKS)]
+        for b in range(BLOCKS):
+            turned = bank(4 + (b + 1) % 2, [P, PACK, P], "turned%d" % b)
+            c, k = divmod(b, CHUNK // P)
+            for j in range(PACK):
+                nc.tensor.transpose(turned[:, j, :], old_raw[c][:, j, k * P : (k + 1) * P], identity[:])
+            nc.scalar.activation(faded[b][:], turned[:], ACT.Copy, scale=fade_cols[:, b : b + 1])
+
+        back_banks = [0, 1, 2, 3, 6, 7, 5, 4]
+        y_bytes = sb.tile([P, U], U8, name="y_bytes", align_bytes=64)
+        words_out = out_1[0].rearrange("p c r -> p (c r)").bitcast(I32)
+        y_bf = [sb.tile([P, CHUNK, PACK], BF16, name="y_bf%d" % c, align_bytes=64) for c in range(CHUNKS)]
+        y_codes = [sb.tile([P, CHUNK], U32, name="y_codes%d" % c, align_bytes=64) for c in range(CHUNKS)]
+
+        def hand_on(c):
+            cols = slice(c * CHUNK, (c + 1) * CHUNK)
+            nc.vector.quantize_mx(y_codes[c][:].bitcast(FP8X4), y_bytes[:, cols], y_bf[c][:].rearrange("p u j -> p (u j)"))
+            nc.sync.dma_start(words_out[:, cols], y_codes[c][:].bitcast(I32))
+
+        for c in range(CHUNKS):
+            cols = slice(c * CHUNK, (c + 1) * CHUNK)
+            y = sb.tile([P, PACK, CHUNK], F32, name="y%d" % c)
+            for pair in range(2):
+                back = bank(back_banks[2 * c + pair], [P, 2, CHUNK], "back%d_%d" % (c, pair))
+                for k in range(2):
+                    for half in range(CHUNK // P):
+                        b = c * (CHUNK // P) + half
+                        nc.tensor.transpose(back[:, k, half * P : (half + 1) * P], faded[b][:, 2 * pair + k, :], identity[:])
+                for k in range(2):
+                    j = 2 * pair + k
+                    nc.vector.tensor_tensor(y[:, j, :], back[:, k, :], placed[j][:, cols], ALU.add)
+            nc.sync.dma_start(out_rows[:, :, cols], y[:])
+            nc.scalar.copy(
+                y_bf[c][:].rearrange("p (a i) j -> p a j i", i=4),
+                y[:].rearrange("p j (a i) -> p a j i", i=4),
+            )
+            if c > 0:
+                hand_on(c - 1)
+        hand_on(CHUNKS - 1)
+        for quad in range(4):
+            nc.scalar.dma_start(
+                out_2[0, 4 * quad : 4 * quad + 4, :].bitcast(I32),
+                y_bytes[32 * quad : 32 * quad + 4, :].bitcast(I32),
+            )

@@ -1,7 +1,6 @@
 from contextlib import ExitStack
 
 import concourse.mybir as mybir
-from concourse.masks import make_identity
 
 D, E, T, I, U, Q = 512, 512, 2048, 256, 1024, 512
 FLOPS = 2 * D * Q * I + 2 * Q * E * I
@@ -29,6 +28,7 @@ def tile_attend_gvaluestore_pl_kernel(tc, query, keys_words, keys_scales, qs, gr
     nc = tc.nc
     with ExitStack() as ctx:
         sb = ctx.enter_context(tc.tile_pool(name="sb", bufs=1))
+        late = ctx.enter_context(tc.tile_pool(name="late", bufs=1))
         ps = ctx.enter_context(tc.psum_pool(name="ps", bufs=1))
 
         def bank(number, shape, name):
@@ -36,19 +36,21 @@ def tile_attend_gvaluestore_pl_kernel(tc, query, keys_words, keys_scales, qs, gr
 
         key_list = sb.tile([P, I // 16], U16, name="key_list")
         place_list = sb.tile([P, I // 16], U16, name="place_list")
-        key_words = sb.tile([P, T], I32, name="key_words")
+        key_words = late.tile([P, T], I32, name="key_words", offset=8 * U - 64)
         key_bytes = sb.tile([P, T], U8, name="key_bytes")
-        fade_rows = sb.tile([P, P], F32, name="fade_rows")
+        fade_runs = sb.tile([P, BLOCKS], F32, name="fade_runs")
         identity = sb.tile([P, P], F32, name="identity")
-        row_scale = sb.tile([P, PACK], F32, name="row_scale")
+        row_scale = late.tile([P, PACK], F32, name="row_scale", offset=16 * U)
         query_raw = [sb.tile([P, PACK, Q // 2], F32, name="query_raw%d" % h) for h in range(2)]
-        grows_raw = [sb.tile([P, PACK, E // 2], F32, name="grows_raw%d" % h) for h in range(2)]
-        old_raw = [sb.tile([P, PACK, CHUNK], F32, name="old_raw%d" % c) for c in range(CHUNKS)]
+        grows_raw = late.tile([P, PACK, E], F32, name="grows_raw", offset=16 * U + 32)
+        zeros = late.tile([P, P], F32, name="zeros", offset=16 * U - 2 * P)
         placed = [sb.tile([P, U], F32, name="placed%d" % j) for j in range(PACK)]
 
-        nc.vector.memset(key_bytes[:].bitcast(I32), 0)
-        nc.gpsimd.memset(fade_rows[:], 0.0)
-        make_identity(nc, identity[:])
+        nc.gpsimd.memset(key_bytes[:].bitcast(I32), 0)
+        nc.gpsimd.memset(zeros[:], 0.0)
+        nc.gpsimd.affine_select(
+            out=identity[:], in_=zeros[:], pattern=[[-1, P]], compare_op=ALU.not_equal, fill=1.0, base=0, channel_multiplier=1
+        )
 
         query_rows = query.rearrange("(p t) q -> p t q", t=PACK)
         grows_rows = grows.rearrange("(p t) e -> p t e", t=PACK)
@@ -56,6 +58,8 @@ def tile_attend_gvaluestore_pl_kernel(tc, query, keys_words, keys_scales, qs, gr
         out_rows = out_0.rearrange("(p j) u -> p j u", j=PACK)
 
         nc.sync.dma_start(key_list[:], offs)
+        nc.sync.dma_start(place_list[:], offs2)
+        nc.sync.dma_start(fade_runs[:], fade.rearrange("o (p b) -> (o p) b", b=BLOCKS))
         for h in range(2):
             nc.sync.dma_start(query_raw[h][:], query_rows[:, :, h * (Q // 2) : (h + 1) * (Q // 2)])
         for quad in range(4):
@@ -64,33 +68,51 @@ def tile_attend_gvaluestore_pl_kernel(tc, query, keys_words, keys_scales, qs, gr
                 keys_scales[0, 4 * quad : 4 * quad + 4, :].bitcast(I32),
             )
         nc.sync.dma_start(key_words[:], keys_words[0].rearrange("p c r -> p (c r)").bitcast(I32))
-        for h in range(2):
-            nc.sync.dma_start(grows_raw[h][:], grows_rows[:, :, h * (E // 2) : (h + 1) * (E // 2)])
+        nc.sync.dma_start(grows_raw[:], grows_rows)
         nc.sync.dma_start(row_scale[:], qs.rearrange("(p r) o -> p (r o)", r=PACK))
-        nc.sync.dma_start(fade_rows[0:BLOCKS, :], fade.rearrange("o (b p) -> (o b) p", p=P))
-        nc.sync.dma_start(place_list[:], offs2)
-        for c in range(CHUNKS):
-            nc.sync.dma_start(old_raw[c][:], old_rows[:, :, c * CHUNK : (c + 1) * CHUNK])
+
+        fade_all = sb.tile([P, U], F32, name="fade_all")
+        fade_cols = sb.tile([P, BLOCKS], F32, name="fade_cols")
+        for g in range(2):
+            spread = bank(4 + g, [P, 4, P], "spread%d" % g)
+            for k in range(4):
+                b = 4 * g + k
+                nc.tensor.transpose(spread[:, k, :], fade_runs[:, b : b + 1].to_broadcast([P, P]), identity[:])
+            nc.scalar.copy(
+                fade_all[:].rearrange("p (n b) -> p n b", b=BLOCKS)[:, :, 4 * g : 4 * g + 4],
+                spread[:].rearrange("p k n -> p n k"),
+            )
+        for g in range(2):
+            turned_fade = bank(6 + g, [P, 4, P], "turned_fade%d" % g)
+            for k in range(4):
+                b = 4 * g + k
+                nc.tensor.transpose(turned_fade[:, k, :], fade_all[:, b * P : (b + 1) * P], identity[:])
+            nc.scalar.copy(fade_cols[:, 4 * g : 4 * g + 4], turned_fade[:, :, 0])
 
         for j in range(PACK):
-            nc.vector.memset(placed[j][:], 0.0)
+            (nc.vector if j < 2 else nc.gpsimd).memset(placed[j][:], 0.0)
 
         def deal(copy, dealt, raw, h):
             copy(
                 dealt[:, :, 64 * h : 64 * (h + 1), :].rearrange("p r s t -> p s t r"),
-                raw[:].rearrange("p t (s r) -> p s t r", r=PACK),
+                raw.rearrange("p t (s r) -> p s t r", r=PACK),
             )
 
         query_dealt = sb.tile([P, PACK, P, PACK], BF16, name="query_dealt", align_bytes=64)
         query_codes = sb.tile([P, Q], U32, name="query_codes", align_bytes=64)
         query_bytes = sb.tile([P, Q], U8, name="query_bytes", align_bytes=64)
-        for h in range(2):
-            deal(nc.vector.tensor_copy, query_dealt, query_raw[h], h)
         listed_words = sb.tile([P, I], U32, name="listed_words", align_bytes=64)
         listed_bytes = sb.tile([P, I], U8, name="listed_bytes", align_bytes=64)
         nc.vector.tensor_copy(listed_bytes[:], key_bytes[:].indirect(key_list[:]))
+        for h in range(2):
+            deal(nc.vector.tensor_copy, query_dealt, query_raw[h][:], h)
         nc.vector.quantize_mx(query_codes[:].bitcast(FP8X4), query_bytes[:], query_dealt[:].rearrange("p r s t -> p (r s t)"))
         nc.vector.tensor_copy(listed_words[:], key_words[:].bitcast(U32).indirect(key_list[:]))
+
+        old_high = late.tile([P, 2, U], F32, name="old_high", offset=0)
+        old_low = late.tile([P, 2, U], F32, name="old_low", offset=8 * U)
+        nc.sync.dma_start(old_high[:], old_rows[:, 2:4, :])
+        nc.sync.dma_start(old_low[:], old_rows[:, 0:2, :])
 
         weights = sb.tile([P, PACK, I], F32, name="weights")
         neg_max = sb.tile([P, PACK], F32, name="neg_max")
@@ -112,15 +134,15 @@ def tile_attend_gvaluestore_pl_kernel(tc, query, keys_words, keys_scales, qs, gr
         grows_dealt = sb.tile([P, PACK, P, PACK], BF16, name="grows_dealt", align_bytes=64)
         grows_codes = sb.tile([P, E], U32, name="grows_codes", align_bytes=64)
         grows_bytes = sb.tile([P, E], U8, name="grows_bytes", align_bytes=64)
-        deal(nc.vector.tensor_copy, grows_dealt, grows_raw[0], 0)
-        deal(nc.scalar.copy, grows_dealt, grows_raw[1], 1)
+        deal(nc.vector.tensor_copy, grows_dealt, grows_raw[:, :, 0 : E // 2], 0)
+        deal(nc.scalar.copy, grows_dealt, grows_raw[:, :, E // 2 : E], 1)
 
         inv_sum = sb.tile([P, PACK], F32, name="inv_sum")
         factor = sb.tile([P, PACK], F32, name="factor")
         nc.vector.reciprocal(inv_sum[:], row_sum[:])
         nc.vector.tensor_tensor(factor[:], inv_sum[:], row_scale[:], ALU.mult)
 
-        w_bf = [sb.tile([P, HALF, PACK], BF16, name="w_bf%d" % h, align_bytes=64) for h in range(2)]
+        w_bf = [sb.tile([P, HALF, PACK], BF16, name="w_bf%d" % h, tag="rounded%d" % h, align_bytes=64) for h in range(2)]
         w_codes = [sb.tile([P, HALF], U32, name="w_codes%d" % h, align_bytes=64) for h in range(2)]
         w_bytes = [sb.tile([P, HALF], U8, name="w_bytes%d" % h, align_bytes=64) for h in range(2)]
         dv = [sb.tile([P, PACK, HALF], F32, name="dv%d" % h) for h in range(2)]
@@ -147,15 +169,22 @@ def tile_attend_gvaluestore_pl_kernel(tc, query, keys_words, keys_scales, qs, gr
                 stop=True,
             )
 
+        def quantise_grows(first, last):
+            cols = slice(first * P, last * P)
+            nc.vector.quantize_mx(
+                grows_codes[:, cols].bitcast(FP8X4), grows_bytes[:, cols], grows_dealt[:, first:last, :, :].rearrange("p r s t -> p (r s t)")
+            )
+
         weigh(0)
-        nc.vector.quantize_mx(grows_codes[:].bitcast(FP8X4), grows_bytes[:], grows_dealt[:].rearrange("p r s t -> p (r s t)"))
+        quantise_grows(0, 2)
         quantise_weights(0)
         weigh(1)
+        quantise_grows(2, 4)
+        quantise_weights(1)
         for j in range(PACK):
             sums = bank(j, [P, HALF], "dv_first%d" % j)
             value_product(sums[:], 0, j)
             nc.scalar.copy(dv[0][:, j, :], sums[:])
-        quantise_weights(1)
         for pair in range(2):
             sums = bank(6 + pair, [P, 2, HALF], "dv_second%d" % pair)
             for k in range(2):
@@ -165,50 +194,93 @@ def tile_attend_gvaluestore_pl_kernel(tc, query, keys_words, keys_scales, qs, gr
             for j in range(PACK):
                 nc.vector.tensor_copy(placed[j][:].indirect(place_list[:, 8 * h : 8 * (h + 1)]), dv[h][:, j, :])
 
-        fade_cols = sb.tile([P, BLOCKS], F32, name="fade_cols")
-        turned_fade = bank(4, [P, P], "turned_fade")
-        nc.tensor.transpose(turned_fade[:], fade_rows[:], identity[:])
-        nc.scalar.copy(fade_cols[:], turned_fade[:, 0:BLOCKS])
+        wide = U // 2
+        per_chunk = CHUNK // P
+        faded = [sb.tile([P, 2, P], F32, name="faded%d" % b) for b in range(BLOCKS)]
+        faded_one = sb.tile([P, BLOCKS // 2, P], F32, name="faded_one")
+        kept = []
+        for c in range(CHUNKS):
+            turned = bank(4 + c % 2, [P, per_chunk, 2, P], "turned%d" % c)
+            for n in range(per_chunk):
+                b = c * per_chunk + n
+                for k in range(2):
+                    nc.tensor.transpose(turned[:, n, k, :], old_high[:, k, b * P : (b + 1) * P], identity[:])
+            for n in range(per_chunk):
+                b = c * per_chunk + n
+                nc.scalar.activation(faded[b][:], turned[:, n, :, :], ACT.Copy, scale=fade_cols[:, b : b + 1])
+        turned = bank(4, [P, BLOCKS // 2, P], "turned_one")
+        for n in range(BLOCKS // 2):
+            b = BLOCKS // 2 + n
+            nc.tensor.transpose(turned[:, n, :], old_low[:, 1, b * P : (b + 1) * P], identity[:])
+        for n in range(BLOCKS // 2):
+            b = BLOCKS // 2 + n
+            nc.scalar.activation(faded_one[:, n, :], turned[:, n, :], ACT.Copy, scale=fade_cols[:, b : b + 1])
+        for c in range(CHUNKS):
+            back = bank(c, [P, 2, CHUNK], "back%d" % c)
+            for k in range(2):
+                for n in range(per_chunk):
+                    nc.tensor.transpose(back[:, k, n * P : (n + 1) * P], faded[c * per_chunk + n][:, k, :], identity[:])
+            kept.append(back)
+        kept_one = bank(6, [P, wide], "back_one")
+        for n in range(BLOCKS // 2):
+            nc.tensor.transpose(kept_one[:, n * P : (n + 1) * P], faded_one[:, n, :], identity[:])
 
-        faded = [sb.tile([P, PACK, P], F32, name="faded%d" % b) for b in range(BLOCKS)]
-        for b in range(BLOCKS):
-            turned = bank(4 + (b + 1) % 2, [P, PACK, P], "turned%d" % b)
-            c, k = divmod(b, CHUNK // P)
-            for j in range(PACK):
-                nc.tensor.transpose(turned[:, j, :], old_raw[c][:, j, k * P : (k + 1) * P], identity[:])
-            nc.scalar.activation(faded[b][:], turned[:], ACT.Copy, scale=fade_cols[:, b : b + 1])
-
-        back_banks = [0, 1, 2, 3, 6, 7, 5, 4]
+        faded_low = sb.tile([P, U + wide], F32, name="faded_low", tag="rounded1", align_bytes=64)
+        y = [sb.tile([P, PACK, wide], F32, name="y%d" % h) for h in range(2)]
         y_bytes = sb.tile([P, U], U8, name="y_bytes", align_bytes=64)
         words_out = out_1[0].rearrange("p c r -> p (c r)").bitcast(I32)
         y_bf = [sb.tile([P, CHUNK, PACK], BF16, name="y_bf%d" % c, align_bytes=64) for c in range(CHUNKS)]
-        y_codes = [sb.tile([P, CHUNK], U32, name="y_codes%d" % c, align_bytes=64) for c in range(CHUNKS)]
+        y_codes = [sb.tile([P, wide], U32, name="y_codes%d" % h, align_bytes=64) for h in range(2)]
+
+        nc.gpsimd.tensor_tensor(faded_low[:, 0:U], old_low[:, 0, :], fade_all[:], ALU.mult)
+        nc.gpsimd.tensor_tensor(faded_low[:, U : U + wide], old_low[:, 1, 0:wide], fade_all[:, 0:wide], ALU.mult)
+        nc.gpsimd.tensor_tensor(y[0][:, 0, :], faded_low[:, 0:wide], placed[0][:, 0:wide], ALU.add)
+        nc.sync.dma_start(out_rows[:, 0, 0:wide], y[0][:, 0, :])
+        nc.gpsimd.tensor_tensor(y[0][:, 1, :], faded_low[:, U : U + wide], placed[1][:, 0:wide], ALU.add)
+        nc.sync.dma_start(out_rows[:, 1, 0:wide], y[0][:, 1, :])
+        nc.gpsimd.tensor_tensor(y[1][:, 0, :], faded_low[:, wide:U], placed[0][:, wide:U], ALU.add)
+        nc.sync.dma_start(out_rows[:, 0, wide:U], y[1][:, 0, :])
+
+        def add_high(c):
+            h, n = divmod(c, 2)
+            for k in range(2):
+                nc.vector.tensor_tensor(
+                    y[h][:, 2 + k, n * CHUNK : (n + 1) * CHUNK], kept[c][:, k, :], placed[2 + k][:, c * CHUNK : (c + 1) * CHUNK], ALU.add
+                )
+
+        def round_chunk(copy, c):
+            h, n = divmod(c, 2)
+            copy(
+                y_bf[c][:].rearrange("p (a i) j -> p a j i", i=4),
+                y[h][:, :, n * CHUNK : (n + 1) * CHUNK].rearrange("p j (a i) -> p a j i", i=4),
+            )
 
         def hand_on(c):
-            cols = slice(c * CHUNK, (c + 1) * CHUNK)
-            nc.vector.quantize_mx(y_codes[c][:].bitcast(FP8X4), y_bytes[:, cols], y_bf[c][:].rearrange("p u j -> p (u j)"))
-            nc.sync.dma_start(words_out[:, cols], y_codes[c][:].bitcast(I32))
-
-        for c in range(CHUNKS):
-            cols = slice(c * CHUNK, (c + 1) * CHUNK)
-            y = sb.tile([P, PACK, CHUNK], F32, name="y%d" % c)
-            for pair in range(2):
-                back = bank(back_banks[2 * c + pair], [P, 2, CHUNK], "back%d_%d" % (c, pair))
-                for k in range(2):
-                    for half in range(CHUNK // P):
-                        b = c * (CHUNK // P) + half
-                        nc.tensor.transpose(back[:, k, half * P : (half + 1) * P], faded[b][:, 2 * pair + k, :], identity[:])
-                for k in range(2):
-                    j = 2 * pair + k
-                    nc.vector.tensor_tensor(y[:, j, :], back[:, k, :], placed[j][:, cols], ALU.add)
-            nc.sync.dma_start(out_rows[:, :, cols], y[:])
-            nc.scalar.copy(
-                y_bf[c][:].rearrange("p (a i) j -> p a j i", i=4),
-                y[:].rearrange("p j (a i) -> p a j i", i=4),
+            h, n = divmod(c, 2)
+            nc.vector.quantize_mx(
+                y_codes[h][:, n * CHUNK : (n + 1) * CHUNK].bitcast(FP8X4),
+                y_bytes[:, c * CHUNK : (c + 1) * CHUNK],
+                y_bf[c][:].rearrange("p u j -> p (u j)"),
             )
-            if c > 0:
-                hand_on(c - 1)
-        hand_on(CHUNKS - 1)
+
+        add_high(0)
+        round_chunk(nc.scalar.copy, 0)
+        add_high(1)
+        nc.sync.dma_start(out_rows[:, 2:4, 0:wide], y[0][:, 2:4, :])
+        round_chunk(nc.scalar.copy, 1)
+        nc.vector.tensor_tensor(y[1][:, 1, :], kept_one[:], placed[1][:, wide:U], ALU.add)
+        nc.sync.dma_start(out_rows[:, 1, wide:U], y[1][:, 1, :])
+        add_high(2)
+        round_chunk(nc.scalar.copy, 2)
+        add_high(3)
+        nc.sync.dma_start(out_rows[:, 2:4, wide:U], y[1][:, 2:4, :])
+        hand_on(0)
+        round_chunk(nc.vector.tensor_copy, 3)
+        hand_on(1)
+        nc.sync.dma_start(words_out[:, 0:wide], y_codes[0][:].bitcast(I32))
+        for c in (2, 3):
+            hand_on(c)
+            nc.sync.dma_start(words_out[:, c * CHUNK : (c + 1) * CHUNK], y_codes[1][:, (c - 2) * CHUNK : (c - 1) * CHUNK].bitcast(I32))
         for quad in range(4):
             nc.scalar.dma_start(
                 out_2[0, 4 * quad : 4 * quad + 4, :].bitcast(I32),

@@ -36,21 +36,28 @@ def tile_attend_gvaluestore_pl_kernel(tc, query, keys_words, keys_scales, qs, gr
 
         key_list = sb.tile([P, I // 16], U16, name="key_list")
         place_list = sb.tile([P, I // 16], U16, name="place_list")
-        key_words = late.tile([P, T], I32, name="key_words", offset=8 * U - 64)
+        key_words = late.tile([P, T], I32, name="key_words", offset=0)
         key_bytes = sb.tile([P, T], U8, name="key_bytes")
         fade_runs = sb.tile([P, BLOCKS], F32, name="fade_runs")
         identity = sb.tile([P, P], F32, name="identity")
-        row_scale = late.tile([P, PACK], F32, name="row_scale", offset=16 * U)
-        query_raw = [sb.tile([P, PACK, Q // 2], F32, name="query_raw%d" % h) for h in range(2)]
-        grows_raw = late.tile([P, PACK, E], F32, name="grows_raw", offset=16 * U + 32)
-        zeros = late.tile([P, P], F32, name="zeros", offset=16 * U - 2 * P)
+        row_scale = late.tile([P, PACK], F32, name="row_scale", offset=4 * T)
+        query_raw = sb.tile([P, PACK, Q], F32, name="query_raw")
+        grows_raw = late.tile([P, PACK, E], F32, name="grows_raw", offset=4 * T + 32)
+        zeros = [late.tile([P, P // 2], F32, name="zeros%d" % g, offset=at - P) for g, at in enumerate((4 * T, 32 * U))]
         placed = [sb.tile([P, U], F32, name="placed%d" % j) for j in range(PACK)]
 
         nc.gpsimd.memset(key_bytes[:].bitcast(I32), 0)
-        nc.gpsimd.memset(zeros[:], 0.0)
-        nc.gpsimd.affine_select(
-            out=identity[:], in_=zeros[:], pattern=[[-1, P]], compare_op=ALU.not_equal, fill=1.0, base=0, channel_multiplier=1
-        )
+        for g in range(2):
+            nc.gpsimd.memset(zeros[g][:], 0.0)
+            nc.gpsimd.affine_select(
+                out=identity[:, g * (P // 2) : (g + 1) * (P // 2)],
+                in_=zeros[g][:],
+                pattern=[[-1, P // 2]],
+                compare_op=ALU.not_equal,
+                fill=1.0,
+                base=-g * (P // 2),
+                channel_multiplier=1,
+            )
 
         query_rows = query.rearrange("(p t) q -> p t q", t=PACK)
         grows_rows = grows.rearrange("(p t) e -> p t e", t=PACK)
@@ -60,8 +67,7 @@ def tile_attend_gvaluestore_pl_kernel(tc, query, keys_words, keys_scales, qs, gr
         nc.sync.dma_start(key_list[:], offs)
         nc.sync.dma_start(place_list[:], offs2)
         nc.sync.dma_start(fade_runs[:], fade.rearrange("o (p b) -> (o p) b", b=BLOCKS))
-        for h in range(2):
-            nc.sync.dma_start(query_raw[h][:], query_rows[:, :, h * (Q // 2) : (h + 1) * (Q // 2)])
+        nc.sync.dma_start(query_raw[:], query_rows)
         for quad in range(4):
             nc.scalar.dma_start(
                 key_bytes[32 * quad : 32 * quad + 4, :].bitcast(I32),
@@ -92,10 +98,10 @@ def tile_attend_gvaluestore_pl_kernel(tc, query, keys_words, keys_scales, qs, gr
         for j in range(PACK):
             (nc.vector if j < 2 else nc.gpsimd).memset(placed[j][:], 0.0)
 
-        def deal(copy, dealt, raw, h):
+        def deal(copy, dealt, raw, first, last):
             copy(
-                dealt[:, :, 64 * h : 64 * (h + 1), :].rearrange("p r s t -> p s t r"),
-                raw.rearrange("p t (s r) -> p s t r", r=PACK),
+                dealt[:, :, first:last, :].rearrange("p r s t -> p s t r"),
+                raw[:, :, PACK * first : PACK * last].rearrange("p t (s r) -> p s t r", r=PACK),
             )
 
         query_dealt = sb.tile([P, PACK, P, PACK], BF16, name="query_dealt", align_bytes=64)
@@ -104,13 +110,13 @@ def tile_attend_gvaluestore_pl_kernel(tc, query, keys_words, keys_scales, qs, gr
         listed_words = sb.tile([P, I], U32, name="listed_words", align_bytes=64)
         listed_bytes = sb.tile([P, I], U8, name="listed_bytes", align_bytes=64)
         nc.vector.tensor_copy(listed_bytes[:], key_bytes[:].indirect(key_list[:]))
-        for h in range(2):
-            deal(nc.vector.tensor_copy, query_dealt, query_raw[h][:], h)
+        deal(nc.vector.tensor_copy, query_dealt, query_raw, 0, 88)
+        deal(nc.scalar.copy, query_dealt, query_raw, 88, P)
         nc.vector.quantize_mx(query_codes[:].bitcast(FP8X4), query_bytes[:], query_dealt[:].rearrange("p r s t -> p (r s t)"))
         nc.vector.tensor_copy(listed_words[:], key_words[:].bitcast(U32).indirect(key_list[:]))
 
-        old_high = late.tile([P, 2, U], F32, name="old_high", offset=0)
-        old_low = late.tile([P, 2, U], F32, name="old_low", offset=8 * U)
+        old_high = late.tile([P, 2, U], F32, name="old_high", offset=24 * U)
+        old_low = late.tile([P, 2, U], F32, name="old_low", offset=32 * U)
         nc.sync.dma_start(old_high[:], old_rows[:, 2:4, :])
         nc.sync.dma_start(old_low[:], old_rows[:, 0:2, :])
 
@@ -134,8 +140,8 @@ def tile_attend_gvaluestore_pl_kernel(tc, query, keys_words, keys_scales, qs, gr
         grows_dealt = sb.tile([P, PACK, P, PACK], BF16, name="grows_dealt", align_bytes=64)
         grows_codes = sb.tile([P, E], U32, name="grows_codes", align_bytes=64)
         grows_bytes = sb.tile([P, E], U8, name="grows_bytes", align_bytes=64)
-        deal(nc.vector.tensor_copy, grows_dealt, grows_raw[:, :, 0 : E // 2], 0)
-        deal(nc.scalar.copy, grows_dealt, grows_raw[:, :, E // 2 : E], 1)
+        deal(nc.vector.tensor_copy, grows_dealt, grows_raw, 0, 64)
+        deal(nc.scalar.copy, grows_dealt, grows_raw, 64, P)
 
         inv_sum = sb.tile([P, PACK], F32, name="inv_sum")
         factor = sb.tile([P, PACK], F32, name="factor")
@@ -200,7 +206,7 @@ def tile_attend_gvaluestore_pl_kernel(tc, query, keys_words, keys_scales, qs, gr
         faded_one = sb.tile([P, BLOCKS // 2, P], F32, name="faded_one")
         kept = []
         for c in range(CHUNKS):
-            turned = bank(4 + c % 2, [P, per_chunk, 2, P], "turned%d" % c)
+            turned = bank(c % 2, [P, per_chunk, 2, P], "turned%d" % c)
             for n in range(per_chunk):
                 b = c * per_chunk + n
                 for k in range(2):
@@ -208,7 +214,7 @@ def tile_attend_gvaluestore_pl_kernel(tc, query, keys_words, keys_scales, qs, gr
             for n in range(per_chunk):
                 b = c * per_chunk + n
                 nc.scalar.activation(faded[b][:], turned[:, n, :, :], ACT.Copy, scale=fade_cols[:, b : b + 1])
-        turned = bank(4, [P, BLOCKS // 2, P], "turned_one")
+        turned = bank(0, [P, BLOCKS // 2, P], "turned_one")
         for n in range(BLOCKS // 2):
             b = BLOCKS // 2 + n
             nc.tensor.transpose(turned[:, n, :], old_low[:, 1, b * P : (b + 1) * P], identity[:])
@@ -216,7 +222,7 @@ def tile_attend_gvaluestore_pl_kernel(tc, query, keys_words, keys_scales, qs, gr
             b = BLOCKS // 2 + n
             nc.scalar.activation(faded_one[:, n, :], turned[:, n, :], ACT.Copy, scale=fade_cols[:, b : b + 1])
         for c in range(CHUNKS):
-            back = bank(c, [P, 2, CHUNK], "back%d" % c)
+            back = bank(2 + c, [P, 2, CHUNK], "back%d" % c)
             for k in range(2):
                 for n in range(per_chunk):
                     nc.tensor.transpose(back[:, k, n * P : (n + 1) * P], faded[c * per_chunk + n][:, k, :], identity[:])
@@ -235,9 +241,9 @@ def tile_attend_gvaluestore_pl_kernel(tc, query, keys_words, keys_scales, qs, gr
         nc.gpsimd.tensor_tensor(faded_low[:, 0:U], old_low[:, 0, :], fade_all[:], ALU.mult)
         nc.gpsimd.tensor_tensor(faded_low[:, U : U + wide], old_low[:, 1, 0:wide], fade_all[:, 0:wide], ALU.mult)
         nc.gpsimd.tensor_tensor(y[0][:, 0, :], faded_low[:, 0:wide], placed[0][:, 0:wide], ALU.add)
-        nc.sync.dma_start(out_rows[:, 0, 0:wide], y[0][:, 0, :])
+        nc.scalar.dma_start(out_rows[:, 0, 0:wide], y[0][:, 0, :])
         nc.gpsimd.tensor_tensor(y[0][:, 1, :], faded_low[:, U : U + wide], placed[1][:, 0:wide], ALU.add)
-        nc.sync.dma_start(out_rows[:, 1, 0:wide], y[0][:, 1, :])
+        nc.scalar.dma_start(out_rows[:, 1, 0:wide], y[0][:, 1, :])
         nc.gpsimd.tensor_tensor(y[1][:, 0, :], faded_low[:, wide:U], placed[0][:, wide:U], ALU.add)
         nc.sync.dma_start(out_rows[:, 0, wide:U], y[1][:, 0, :])
 
@@ -247,6 +253,7 @@ def tile_attend_gvaluestore_pl_kernel(tc, query, keys_words, keys_scales, qs, gr
                 nc.vector.tensor_tensor(
                     y[h][:, 2 + k, n * CHUNK : (n + 1) * CHUNK], kept[c][:, k, :], placed[2 + k][:, c * CHUNK : (c + 1) * CHUNK], ALU.add
                 )
+            nc.sync.dma_start(out_rows[:, 2:4, c * CHUNK : (c + 1) * CHUNK], y[h][:, 2:4, n * CHUNK : (n + 1) * CHUNK])
 
         def round_chunk(copy, c):
             h, n = divmod(c, 2)
@@ -266,14 +273,12 @@ def tile_attend_gvaluestore_pl_kernel(tc, query, keys_words, keys_scales, qs, gr
         add_high(0)
         round_chunk(nc.scalar.copy, 0)
         add_high(1)
-        nc.sync.dma_start(out_rows[:, 2:4, 0:wide], y[0][:, 2:4, :])
         round_chunk(nc.scalar.copy, 1)
         nc.vector.tensor_tensor(y[1][:, 1, :], kept_one[:], placed[1][:, wide:U], ALU.add)
         nc.sync.dma_start(out_rows[:, 1, wide:U], y[1][:, 1, :])
         add_high(2)
         round_chunk(nc.scalar.copy, 2)
         add_high(3)
-        nc.sync.dma_start(out_rows[:, 2:4, wide:U], y[1][:, 2:4, :])
         hand_on(0)
         round_chunk(nc.vector.tensor_copy, 3)
         hand_on(1)
@@ -282,7 +287,7 @@ def tile_attend_gvaluestore_pl_kernel(tc, query, keys_words, keys_scales, qs, gr
             hand_on(c)
             nc.sync.dma_start(words_out[:, c * CHUNK : (c + 1) * CHUNK], y_codes[1][:, (c - 2) * CHUNK : (c - 1) * CHUNK].bitcast(I32))
         for quad in range(4):
-            nc.scalar.dma_start(
+            (nc.scalar if quad < 3 else nc.sync).dma_start(
                 out_2[0, 4 * quad : 4 * quad + 4, :].bitcast(I32),
                 y_bytes[32 * quad : 32 * quad + 4, :].bitcast(I32),
             )

@@ -18,10 +18,22 @@ AXIS = mybir.AxisListType
 
 P = 128
 PACK = 4
+RUN = 4
+QUADS = 4
+PER_BANK = 4
+LIST_ROWS = 16
 HALF = I // 2
+WIDE = U // 2
 CHUNK = 256
 CHUNKS = U // CHUNK
 BLOCKS = U // P
+PER_CHUNK = CHUNK // P
+QUERY_ON_VECTOR = 88
+GROWS_ON_VECTOR = 64
+
+FIRST_SEAM = 4 * T
+SCALE_SLOT = 32
+SECOND_SEAM = 32 * U
 
 
 def tile_attend_gvaluestore_pl_kernel(tc, query, keys_words, keys_scales, qs, grows, old, fade, offs, offs2, out_0, out_1, out_2):
@@ -34,16 +46,16 @@ def tile_attend_gvaluestore_pl_kernel(tc, query, keys_words, keys_scales, qs, gr
         def bank(number, shape, name):
             return ps.tile(shape, F32, name=name, tag="bank%d" % number)
 
-        key_list = sb.tile([P, I // 16], U16, name="key_list")
-        place_list = sb.tile([P, I // 16], U16, name="place_list")
+        key_list = sb.tile([P, I // LIST_ROWS], U16, name="key_list")
+        place_list = sb.tile([P, I // LIST_ROWS], U16, name="place_list")
         key_words = late.tile([P, T], I32, name="key_words", offset=0)
         key_bytes = sb.tile([P, T], U8, name="key_bytes")
         fade_runs = sb.tile([P, BLOCKS], F32, name="fade_runs")
         identity = sb.tile([P, P], F32, name="identity")
-        row_scale = late.tile([P, PACK], F32, name="row_scale", offset=4 * T)
+        row_scale = late.tile([P, PACK], F32, name="row_scale", offset=FIRST_SEAM)
         query_raw = sb.tile([P, PACK, Q], F32, name="query_raw")
-        grows_raw = late.tile([P, PACK, E], F32, name="grows_raw", offset=4 * T + 32)
-        zeros = [late.tile([P, P // 2], F32, name="zeros%d" % g, offset=at - P) for g, at in enumerate((4 * T, 32 * U))]
+        grows_raw = late.tile([P, PACK, E], F32, name="grows_raw", offset=FIRST_SEAM + SCALE_SLOT)
+        zeros = [late.tile([P, P // 2], F32, name="zeros%d" % g, offset=seam - P) for g, seam in enumerate((FIRST_SEAM, SECOND_SEAM))]
         placed = [sb.tile([P, U], F32, name="placed%d" % j) for j in range(PACK)]
 
         nc.gpsimd.memset(key_bytes[:].bitcast(I32), 0)
@@ -68,7 +80,7 @@ def tile_attend_gvaluestore_pl_kernel(tc, query, keys_words, keys_scales, qs, gr
         nc.sync.dma_start(place_list[:], offs2)
         nc.sync.dma_start(fade_runs[:], fade.rearrange("o (p b) -> (o p) b", b=BLOCKS))
         nc.sync.dma_start(query_raw[:], query_rows)
-        for quad in range(4):
+        for quad in range(QUADS):
             nc.scalar.dma_start(
                 key_bytes[32 * quad : 32 * quad + 4, :].bitcast(I32),
                 keys_scales[0, 4 * quad : 4 * quad + 4, :].bitcast(I32),
@@ -79,21 +91,21 @@ def tile_attend_gvaluestore_pl_kernel(tc, query, keys_words, keys_scales, qs, gr
 
         fade_all = sb.tile([P, U], F32, name="fade_all")
         fade_cols = sb.tile([P, BLOCKS], F32, name="fade_cols")
-        for g in range(2):
-            spread = bank(4 + g, [P, 4, P], "spread%d" % g)
-            for k in range(4):
-                b = 4 * g + k
+        for g in range(BLOCKS // PER_BANK):
+            spread = bank(4 + g, [P, PER_BANK, P], "spread%d" % g)
+            for k in range(PER_BANK):
+                b = PER_BANK * g + k
                 nc.tensor.transpose(spread[:, k, :], fade_runs[:, b : b + 1].to_broadcast([P, P]), identity[:])
             nc.scalar.copy(
-                fade_all[:].rearrange("p (n b) -> p n b", b=BLOCKS)[:, :, 4 * g : 4 * g + 4],
+                fade_all[:].rearrange("p (n b) -> p n b", b=BLOCKS)[:, :, PER_BANK * g : PER_BANK * (g + 1)],
                 spread[:].rearrange("p k n -> p n k"),
             )
-        for g in range(2):
-            turned_fade = bank(6 + g, [P, 4, P], "turned_fade%d" % g)
-            for k in range(4):
-                b = 4 * g + k
+        for g in range(BLOCKS // PER_BANK):
+            turned_fade = bank(6 + g, [P, PER_BANK, P], "turned_fade%d" % g)
+            for k in range(PER_BANK):
+                b = PER_BANK * g + k
                 nc.tensor.transpose(turned_fade[:, k, :], fade_all[:, b * P : (b + 1) * P], identity[:])
-            nc.scalar.copy(fade_cols[:, 4 * g : 4 * g + 4], turned_fade[:, :, 0])
+            nc.scalar.copy(fade_cols[:, PER_BANK * g : PER_BANK * (g + 1)], turned_fade[:, :, 0])
 
         for j in range(PACK):
             (nc.vector if j < 2 else nc.gpsimd).memset(placed[j][:], 0.0)
@@ -110,17 +122,17 @@ def tile_attend_gvaluestore_pl_kernel(tc, query, keys_words, keys_scales, qs, gr
         listed_words = sb.tile([P, I], U32, name="listed_words", align_bytes=64)
         listed_bytes = sb.tile([P, I], U8, name="listed_bytes", align_bytes=64)
         nc.vector.tensor_copy(listed_bytes[:], key_bytes[:].indirect(key_list[:]))
-        deal(nc.vector.tensor_copy, query_dealt, query_raw, 0, 88)
-        deal(nc.scalar.copy, query_dealt, query_raw, 88, P)
+        deal(nc.vector.tensor_copy, query_dealt, query_raw, 0, QUERY_ON_VECTOR)
+        deal(nc.scalar.copy, query_dealt, query_raw, QUERY_ON_VECTOR, P)
         nc.vector.quantize_mx(query_codes[:].bitcast(FP8X4), query_bytes[:], query_dealt[:].rearrange("p r s t -> p (r s t)"))
         nc.vector.tensor_copy(listed_words[:], key_words[:].bitcast(U32).indirect(key_list[:]))
 
-        old_high = late.tile([P, 2, U], F32, name="old_high", offset=24 * U)
-        old_low = late.tile([P, 2, U], F32, name="old_low", offset=32 * U)
+        old_high = late.tile([P, 2, U], F32, name="old_high", offset=SECOND_SEAM - 2 * U * 4)
+        old_low = late.tile([P, 2, U], F32, name="old_low", offset=SECOND_SEAM)
         nc.sync.dma_start(old_high[:], old_rows[:, 2:4, :])
         nc.sync.dma_start(old_low[:], old_rows[:, 0:2, :])
 
-        weights = sb.tile([P, PACK, I], F32, name="weights")
+        exps = sb.tile([P, PACK, I], F32, name="weights")
         neg_max = sb.tile([P, PACK], F32, name="neg_max")
         row_sum = sb.tile([P, PACK], F32, name="row_sum")
         for r in range(PACK):
@@ -135,13 +147,13 @@ def tile_attend_gvaluestore_pl_kernel(tc, query, keys_words, keys_scales, qs, gr
                 stop=True,
             )
             nc.vector.tensor_reduce(neg_max[:, r : r + 1], scores[:], AXIS.X, ALU.max, negate=True)
-            nc.scalar.activation(weights[:, r, :], scores[:], ACT.Exp, bias=neg_max[:, r : r + 1], accum_out=row_sum[:, r : r + 1])
+            nc.scalar.activation(exps[:, r, :], scores[:], ACT.Exp, bias=neg_max[:, r : r + 1], accum_out=row_sum[:, r : r + 1])
 
         grows_dealt = sb.tile([P, PACK, P, PACK], BF16, name="grows_dealt", align_bytes=64)
         grows_codes = sb.tile([P, E], U32, name="grows_codes", align_bytes=64)
         grows_bytes = sb.tile([P, E], U8, name="grows_bytes", align_bytes=64)
-        deal(nc.vector.tensor_copy, grows_dealt, grows_raw, 0, 64)
-        deal(nc.scalar.copy, grows_dealt, grows_raw, 64, P)
+        deal(nc.vector.tensor_copy, grows_dealt, grows_raw, 0, GROWS_ON_VECTOR)
+        deal(nc.scalar.copy, grows_dealt, grows_raw, GROWS_ON_VECTOR, P)
 
         inv_sum = sb.tile([P, PACK], F32, name="inv_sum")
         factor = sb.tile([P, PACK], F32, name="factor")
@@ -155,9 +167,9 @@ def tile_attend_gvaluestore_pl_kernel(tc, query, keys_words, keys_scales, qs, gr
 
         def weigh(h):
             nc.vector.tensor_tensor(
-                w_bf[h][:].rearrange("p (c i) r -> p c r i", i=4),
-                weights[:, :, h * HALF : (h + 1) * HALF].rearrange("p r (c i) -> p c r i", i=4),
-                factor[:].unsqueeze(1).unsqueeze(3).broadcast_to([P, HALF // 4, PACK, 4]),
+                w_bf[h][:].rearrange("p (c i) r -> p c r i", i=RUN),
+                exps[:, :, h * HALF : (h + 1) * HALF].rearrange("p r (c i) -> p c r i", i=RUN),
+                factor[:].unsqueeze(1).unsqueeze(3).broadcast_to([P, HALF // RUN, PACK, RUN]),
                 ALU.mult,
             )
 
@@ -181,12 +193,11 @@ def tile_attend_gvaluestore_pl_kernel(tc, query, keys_words, keys_scales, qs, gr
                 grows_codes[:, cols].bitcast(FP8X4), grows_bytes[:, cols], grows_dealt[:, first:last, :, :].rearrange("p r s t -> p (r s t)")
             )
 
-        weigh(0)
-        quantise_grows(0, 2)
-        quantise_weights(0)
-        weigh(1)
-        quantise_grows(2, 4)
-        quantise_weights(1)
+        for h in range(2):
+            weigh(h)
+            quantise_grows(2 * h, 2 * h + 2)
+            quantise_weights(h)
+
         for j in range(PACK):
             sums = bank(j, [P, HALF], "dv_first%d" % j)
             value_product(sums[:], 0, j)
@@ -196,56 +207,55 @@ def tile_attend_gvaluestore_pl_kernel(tc, query, keys_words, keys_scales, qs, gr
             for k in range(2):
                 value_product(sums[:, k, :], 1, 2 * pair + k)
             nc.scalar.copy(dv[1][:, 2 * pair : 2 * pair + 2, :], sums[:])
+        half_cols = HALF // LIST_ROWS
         for h in range(2):
             for j in range(PACK):
-                nc.vector.tensor_copy(placed[j][:].indirect(place_list[:, 8 * h : 8 * (h + 1)]), dv[h][:, j, :])
+                nc.vector.tensor_copy(placed[j][:].indirect(place_list[:, half_cols * h : half_cols * (h + 1)]), dv[h][:, j, :])
 
-        wide = U // 2
-        per_chunk = CHUNK // P
         faded = [sb.tile([P, 2, P], F32, name="faded%d" % b) for b in range(BLOCKS)]
         faded_one = sb.tile([P, BLOCKS // 2, P], F32, name="faded_one")
         kept = []
         for c in range(CHUNKS):
-            turned = bank(c % 2, [P, per_chunk, 2, P], "turned%d" % c)
-            for n in range(per_chunk):
-                b = c * per_chunk + n
+            turned = bank(c % 2 if c > 0 else 4, [P, PER_CHUNK, 2, P], "turned%d" % c)
+            for n in range(PER_CHUNK):
+                b = c * PER_CHUNK + n
                 for k in range(2):
                     nc.tensor.transpose(turned[:, n, k, :], old_high[:, k, b * P : (b + 1) * P], identity[:])
-            for n in range(per_chunk):
-                b = c * per_chunk + n
+            for n in range(PER_CHUNK):
+                b = c * PER_CHUNK + n
                 nc.scalar.activation(faded[b][:], turned[:, n, :, :], ACT.Copy, scale=fade_cols[:, b : b + 1])
-        turned = bank(0, [P, BLOCKS // 2, P], "turned_one")
+        turned_one = bank(0, [P, BLOCKS // 2, P], "turned_one")
         for n in range(BLOCKS // 2):
             b = BLOCKS // 2 + n
-            nc.tensor.transpose(turned[:, n, :], old_low[:, 1, b * P : (b + 1) * P], identity[:])
+            nc.tensor.transpose(turned_one[:, n, :], old_low[:, 1, b * P : (b + 1) * P], identity[:])
         for n in range(BLOCKS // 2):
             b = BLOCKS // 2 + n
-            nc.scalar.activation(faded_one[:, n, :], turned[:, n, :], ACT.Copy, scale=fade_cols[:, b : b + 1])
+            nc.scalar.activation(faded_one[:, n, :], turned_one[:, n, :], ACT.Copy, scale=fade_cols[:, b : b + 1])
         for c in range(CHUNKS):
             back = bank(2 + c, [P, 2, CHUNK], "back%d" % c)
             for k in range(2):
-                for n in range(per_chunk):
-                    nc.tensor.transpose(back[:, k, n * P : (n + 1) * P], faded[c * per_chunk + n][:, k, :], identity[:])
+                for n in range(PER_CHUNK):
+                    nc.tensor.transpose(back[:, k, n * P : (n + 1) * P], faded[c * PER_CHUNK + n][:, k, :], identity[:])
             kept.append(back)
-        kept_one = bank(6, [P, wide], "back_one")
+        kept_one = bank(6, [P, WIDE], "back_one")
         for n in range(BLOCKS // 2):
             nc.tensor.transpose(kept_one[:, n * P : (n + 1) * P], faded_one[:, n, :], identity[:])
 
-        faded_low = sb.tile([P, U + wide], F32, name="faded_low", tag="rounded1", align_bytes=64)
-        y = [sb.tile([P, PACK, wide], F32, name="y%d" % h) for h in range(2)]
+        faded_low = sb.tile([P, U + WIDE], F32, name="faded_low", tag="rounded1", align_bytes=64)
+        y = [sb.tile([P, PACK, WIDE], F32, name="y%d" % h) for h in range(2)]
         y_bytes = sb.tile([P, U], U8, name="y_bytes", align_bytes=64)
         words_out = out_1[0].rearrange("p c r -> p (c r)").bitcast(I32)
         y_bf = [sb.tile([P, CHUNK, PACK], BF16, name="y_bf%d" % c, align_bytes=64) for c in range(CHUNKS)]
-        y_codes = [sb.tile([P, wide], U32, name="y_codes%d" % h, align_bytes=64) for h in range(2)]
+        y_codes = [sb.tile([P, WIDE], U32, name="y_codes%d" % h, align_bytes=64) for h in range(2)]
 
         nc.gpsimd.tensor_tensor(faded_low[:, 0:U], old_low[:, 0, :], fade_all[:], ALU.mult)
-        nc.gpsimd.tensor_tensor(faded_low[:, U : U + wide], old_low[:, 1, 0:wide], fade_all[:, 0:wide], ALU.mult)
-        nc.gpsimd.tensor_tensor(y[0][:, 0, :], faded_low[:, 0:wide], placed[0][:, 0:wide], ALU.add)
-        nc.scalar.dma_start(out_rows[:, 0, 0:wide], y[0][:, 0, :])
-        nc.gpsimd.tensor_tensor(y[0][:, 1, :], faded_low[:, U : U + wide], placed[1][:, 0:wide], ALU.add)
-        nc.scalar.dma_start(out_rows[:, 1, 0:wide], y[0][:, 1, :])
-        nc.gpsimd.tensor_tensor(y[1][:, 0, :], faded_low[:, wide:U], placed[0][:, wide:U], ALU.add)
-        nc.sync.dma_start(out_rows[:, 0, wide:U], y[1][:, 0, :])
+        nc.gpsimd.tensor_tensor(faded_low[:, U : U + WIDE], old_low[:, 1, 0:WIDE], fade_all[:, 0:WIDE], ALU.mult)
+        nc.gpsimd.tensor_tensor(y[0][:, 0, :], faded_low[:, 0:WIDE], placed[0][:, 0:WIDE], ALU.add)
+        nc.scalar.dma_start(out_rows[:, 0, 0:WIDE], y[0][:, 0, :])
+        nc.gpsimd.tensor_tensor(y[0][:, 1, :], faded_low[:, U : U + WIDE], placed[1][:, 0:WIDE], ALU.add)
+        nc.scalar.dma_start(out_rows[:, 1, 0:WIDE], y[0][:, 1, :])
+        nc.gpsimd.tensor_tensor(y[1][:, 0, :], faded_low[:, WIDE:U], placed[0][:, WIDE:U], ALU.add)
+        nc.sync.dma_start(out_rows[:, 0, WIDE:U], y[1][:, 0, :])
 
         def add_high(c):
             h, n = divmod(c, 2)
@@ -258,11 +268,11 @@ def tile_attend_gvaluestore_pl_kernel(tc, query, keys_words, keys_scales, qs, gr
         def round_chunk(copy, c):
             h, n = divmod(c, 2)
             copy(
-                y_bf[c][:].rearrange("p (a i) j -> p a j i", i=4),
-                y[h][:, :, n * CHUNK : (n + 1) * CHUNK].rearrange("p j (a i) -> p a j i", i=4),
+                y_bf[c][:].rearrange("p (a i) j -> p a j i", i=RUN),
+                y[h][:, :, n * CHUNK : (n + 1) * CHUNK].rearrange("p j (a i) -> p a j i", i=RUN),
             )
 
-        def hand_on(c):
+        def quantise_chunk(c):
             h, n = divmod(c, 2)
             nc.vector.quantize_mx(
                 y_codes[h][:, n * CHUNK : (n + 1) * CHUNK].bitcast(FP8X4),
@@ -274,20 +284,21 @@ def tile_attend_gvaluestore_pl_kernel(tc, query, keys_words, keys_scales, qs, gr
         round_chunk(nc.scalar.copy, 0)
         add_high(1)
         round_chunk(nc.scalar.copy, 1)
-        nc.vector.tensor_tensor(y[1][:, 1, :], kept_one[:], placed[1][:, wide:U], ALU.add)
-        nc.sync.dma_start(out_rows[:, 1, wide:U], y[1][:, 1, :])
+        nc.vector.tensor_tensor(y[1][:, 1, :], kept_one[:], placed[1][:, WIDE:U], ALU.add)
+        nc.sync.dma_start(out_rows[:, 1, WIDE:U], y[1][:, 1, :])
         add_high(2)
         round_chunk(nc.scalar.copy, 2)
         add_high(3)
-        hand_on(0)
+        quantise_chunk(0)
         round_chunk(nc.vector.tensor_copy, 3)
-        hand_on(1)
-        nc.sync.dma_start(words_out[:, 0:wide], y_codes[0][:].bitcast(I32))
-        for c in (2, 3):
-            hand_on(c)
-            nc.sync.dma_start(words_out[:, c * CHUNK : (c + 1) * CHUNK], y_codes[1][:, (c - 2) * CHUNK : (c - 1) * CHUNK].bitcast(I32))
-        for quad in range(4):
-            (nc.scalar if quad < 3 else nc.sync).dma_start(
+        quantise_chunk(1)
+        nc.sync.dma_start(words_out[:, 0:WIDE], y_codes[0][:].bitcast(I32))
+        for n in range(2):
+            c = 2 + n
+            quantise_chunk(c)
+            nc.sync.dma_start(words_out[:, c * CHUNK : (c + 1) * CHUNK], y_codes[1][:, n * CHUNK : (n + 1) * CHUNK].bitcast(I32))
+        for quad in range(QUADS):
+            (nc.scalar if quad < QUADS - 1 else nc.sync).dma_start(
                 out_2[0, 4 * quad : 4 * quad + 4, :].bitcast(I32),
                 y_bytes[32 * quad : 32 * quad + 4, :].bitcast(I32),
             )

from contextlib import ExitStack

import concourse.mybir as mybir

D, E, T, I, U, Q = 512, 512, 2048, 256, 1024, 512
FLOPS = 2 * D * Q * I + 2 * Q * E * I

F32 = mybir.dt.float32
BF16 = mybir.dt.bfloat16
I32 = mybir.dt.int32
U32 = mybir.dt.uint32
U16 = mybir.dt.uint16
U8 = mybir.dt.uint8
FP8X4 = mybir.dt.float8_e4m3fn_x4
ALU = mybir.AluOpType
ACT = mybir.ActivationFunctionType
AXIS = mybir.AxisListType

P = 128
PACK = 4
RUN = 4
QUADS = 4
PER_BANK = 4
LIST_ROWS = 16
HALF = I // 2
WIDE = U // 2
CHUNK = 256
CHUNKS = U // CHUNK
BLOCKS = U // P
PER_CHUNK = CHUNK // P
QUERY_ON_VECTOR = 88
GROWS_ON_VECTOR = 64

FIRST_SEAM = 4 * T
SCALE_SLOT = 32
SECOND_SEAM = 32 * U


def tile_attend_gvaluestore_pl_kernel(tc, query, keys_words, keys_scales, qs, grows, old, fade, offs, offs2, out_0, out_1, out_2):
    nc = tc.nc
    with ExitStack() as ctx:
        sb = ctx.enter_context(tc.tile_pool(name="sb", bufs=1))
        late = ctx.enter_context(tc.tile_pool(name="late", bufs=1))
        ps = ctx.enter_context(tc.psum_pool(name="ps", bufs=1))

        def bank(number, shape, name):
            return ps.tile(shape, F32, name=name, tag="bank%d" % number)

        key_list = sb.tile([P, I // LIST_ROWS], U16, name="key_list")
        place_list = sb.tile([P, I // LIST_ROWS], U16, name="place_list")
        key_words = late.tile([P, T], I32, name="key_words", offset=0)
        key_bytes = sb.tile([P, T], U8, name="key_bytes")
        fade_runs = sb.tile([P, BLOCKS], F32, name="fade_runs")
        identity = sb.tile([P, P], F32, name="identity")
        row_scale = late.tile([P, PACK], F32, name="row_scale", offset=FIRST_SEAM)
        query_raw = sb.tile([P, PACK, Q], F32, name="query_raw")
        grows_raw = late.tile([P, PACK, E], F32, name="grows_raw", offset=FIRST_SEAM + SCALE_SLOT)
        zeros = [late.tile([P, P // 2], F32, name="zeros%d" % g, offset=seam - P) for g, seam in enumerate((FIRST_SEAM, SECOND_SEAM))]
        placed = [sb.tile([P, U], F32, name="placed%d" % j) for j in range(PACK)]

        nc.gpsimd.memset(key_bytes[:].bitcast(I32), 0)
        for g in range(2):
            nc.gpsimd.memset(zeros[g][:], 0.0)
            nc.gpsimd.affine_select(
                out=identity[:, g * (P // 2) : (g + 1) * (P // 2)],
                in_=zeros[g][:],
                pattern=[[-1, P // 2]],
                compare_op=ALU.not_equal,
                fill=1.0,
                base=-g * (P // 2),
                channel_multiplier=1,
            )

        query_rows = query.rearrange("(p t) q -> p t q", t=PACK)
        grows_rows = grows.rearrange("(p t) e -> p t e", t=PACK)
        old_rows = old.rearrange("(p j) u -> p j u", j=PACK)
        out_rows = out_0.rearrange("(p j) u -> p j u", j=PACK)

        nc.sync.dma_start(key_list[:], offs)
        nc.sync.dma_start(place_list[:], offs2)
        nc.sync.dma_start(fade_runs[:], fade.rearrange("o (p b) -> (o p) b", b=BLOCKS))
        nc.sync.dma_start(query_raw[:], query_rows)
        for quad in range(QUADS):
            nc.scalar.dma_start(
                key_bytes[32 * quad : 32 * quad + 4, :].bitcast(I32),
                keys_scales[0, 4 * quad : 4 * quad + 4, :].bitcast(I32),
            )
        nc.sync.dma_start(key_words[:], keys_words[0].rearrange("p c r -> p (c r)").bitcast(I32))
        nc.sync.dma_start(grows_raw[:], grows_rows)
        nc.sync.dma_start(row_scale[:], qs.rearrange("(p r) o -> p (r o)", r=PACK))

        fade_all = sb.tile([P, U], F32, name="fade_all")
        fade_cols = sb.tile([P, BLOCKS], F32, name="fade_cols")
        for g in range(BLOCKS // PER_BANK):
            spread = bank(4 + g, [P, PER_BANK, P], "spread%d" % g)
            for k in range(PER_BANK):
                b = PER_BANK * g + k
                nc.tensor.transpose(spread[:, k, :], fade_runs[:, b : b + 1].to_broadcast([P, P]), identity[:])
            nc.scalar.copy(
                fade_all[:].rearrange("p (n b) -> p n b", b=BLOCKS)[:, :, PER_BANK * g : PER_BANK * (g + 1)],
                spread[:].rearrange("p k n -> p n k"),
            )
        for g in range(BLOCKS // PER_BANK):
            turned_fade = bank(6 + g, [P, PER_BANK, P], "turned_fade%d" % g)
            for k in range(PER_BANK):
                b = PER_BANK * g + k
                nc.tensor.transpose(turned_fade[:, k, :], fade_all[:, b * P : (b + 1) * P], identity[:])
            nc.scalar.copy(fade_cols[:, PER_BANK * g : PER_BANK * (g + 1)], turned_fade[:, :, 0])

        for j in range(PACK):
            (nc.vector if j < 2 else nc.gpsimd).memset(placed[j][:], 0.0)

        def deal(copy, dealt, raw, first, last):
            copy(
                dealt[:, :, first:last, :].rearrange("p r s t -> p s t r"),
                raw[:, :, PACK * first : PACK * last].rearrange("p t (s r) -> p s t r", r=PACK),
            )

        query_dealt = sb.tile([P, PACK, P, PACK], BF16, name="query_dealt", align_bytes=64)
        query_codes = sb.tile([P, Q], U32, name="query_codes", align_bytes=64)
        query_bytes = sb.tile([P, Q], U8, name="query_bytes", align_bytes=64)
        listed_words = sb.tile([P, I], U32, name="listed_words", align_bytes=64)
        listed_bytes = sb.tile([P, I], U8, name="listed_bytes", align_bytes=64)
        nc.vector.tensor_copy(listed_bytes[:], key_bytes[:].indirect(key_list[:]))
        deal(nc.vector.tensor_copy, query_dealt, query_raw, 0, QUERY_ON_VECTOR)
        deal(nc.scalar.copy, query_dealt, query_raw, QUERY_ON_VECTOR, P)
        nc.vector.quantize_mx(query_codes[:].bitcast(FP8X4), query_bytes[:], query_dealt[:].rearrange("p r s t -> p (r s t)"))
        nc.vector.tensor_copy(listed_words[:], key_words[:].bitcast(U32).indirect(key_list[:]))

        old_high = late.tile([P, 2, U], F32, name="old_high", offset=SECOND_SEAM - 2 * U * 4)
        old_low = late.tile([P, 2, U], F32, name="old_low", offset=SECOND_SEAM)
        nc.sync.dma_start(old_high[:], old_rows[:, 2:4, :])
        nc.sync.dma_start(old_low[:], old_rows[:, 0:2, :])

        exps = sb.tile([P, PACK, I], F32, name="weights")
        neg_max = sb.tile([P, PACK], F32, name="neg_max")
        row_sum = sb.tile([P, PACK], F32, name="row_sum")
        for r in range(PACK):
            scores = bank(r, [P, I], "scores%d" % r)
            nc.tensor.matmul_mx(
                scores[:],
                lhsT=query_codes[:, r * P : (r + 1) * P].bitcast(FP8X4),
                lhsT_scale=query_bytes[:, r * P : (r + 1) * P],
                rhs=listed_words[:].bitcast(FP8X4),
                rhs_scale=listed_bytes[:],
                start=True,
                stop=True,
            )
            nc.vector.tensor_reduce(neg_max[:, r : r + 1], scores[:], AXIS.X, ALU.max, negate=True)
            nc.scalar.activation(exps[:, r, :], scores[:], ACT.Exp, bias=neg_max[:, r : r + 1], accum_out=row_sum[:, r : r + 1])

        grows_dealt = sb.tile([P, PACK, P, PACK], BF16, name="grows_dealt", align_bytes=64)
        grows_codes = sb.tile([P, E], U32, name="grows_codes", align_bytes=64)
        grows_bytes = sb.tile([P, E], U8, name="grows_bytes", align_bytes=64)
        deal(nc.vector.tensor_copy, grows_dealt, grows_raw, 0, GROWS_ON_VECTOR)
        deal(nc.scalar.copy, grows_dealt, grows_raw, GROWS_ON_VECTOR, P)

        inv_sum = sb.tile([P, PACK], F32, name="inv_sum")
        factor = sb.tile([P, PACK], F32, name="factor")
        nc.vector.reciprocal(inv_sum[:], row_sum[:])
        nc.vector.tensor_tensor(factor[:], inv_sum[:], row_scale[:], ALU.mult)

        w_bf = [sb.tile([P, HALF, PACK], BF16, name="w_bf%d" % h, tag="rounded%d" % h, align_bytes=64) for h in range(2)]
        w_codes = [sb.tile([P, HALF], U32, name="w_codes%d" % h, align_bytes=64) for h in range(2)]
        w_bytes = [sb.tile([P, HALF], U8, name="w_bytes%d" % h, align_bytes=64) for h in range(2)]
        dv = [sb.tile([P, PACK, HALF], F32, name="dv%d" % h) for h in range(2)]

        def weigh(h):
            nc.vector.tensor_tensor(
                w_bf[h][:].rearrange("p (c i) r -> p c r i", i=RUN),
                exps[:, :, h * HALF : (h + 1) * HALF].rearrange("p r (c i) -> p c r i", i=RUN),
                factor[:].unsqueeze(1).unsqueeze(3).broadcast_to([P, HALF // RUN, PACK, RUN]),
                ALU.mult,
            )

        def quantise_weights(h):
            nc.vector.quantize_mx(w_codes[h][:].bitcast(FP8X4), w_bytes[h][:], w_bf[h][:].rearrange("p i r -> p (i r)"))

        def value_product(out, h, j):
            nc.tensor.matmul_mx(
                out,
                lhsT=grows_codes[:, j * P : (j + 1) * P].bitcast(FP8X4),
                lhsT_scale=grows_bytes[:, j * P : (j + 1) * P],
                rhs=w_codes[h][:].bitcast(FP8X4),
                rhs_scale=w_bytes[h][:],
                start=True,
                stop=True,
            )

        def quantise_grows(first, last):
            cols = slice(first * P, last * P)
            nc.vector.quantize_mx(
                grows_codes[:, cols].bitcast(FP8X4), grows_bytes[:, cols], grows_dealt[:, first:last, :, :].rearrange("p r s t -> p (r s t)")
            )

        for h in range(2):
            weigh(h)
            quantise_grows(2 * h, 2 * h + 2)
            quantise_weights(h)

        for j in range(PACK):
            sums = bank(j, [P, HALF], "dv_first%d" % j)
            value_product(sums[:], 0, j)
            nc.scalar.copy(dv[0][:, j, :], sums[:])
        for pair in range(2):
            sums = bank(6 + pair, [P, 2, HALF], "dv_second%d" % pair)
            for k in range(2):
                value_product(sums[:, k, :], 1, 2 * pair + k)
            nc.scalar.copy(dv[1][:, 2 * pair : 2 * pair + 2, :], sums[:])
        half_cols = HALF // LIST_ROWS
        for h in range(2):
            for j in range(PACK):
                nc.vector.tensor_copy(placed[j][:].indirect(place_list[:, half_cols * h : half_cols * (h + 1)]), dv[h][:, j, :])

        faded = [sb.tile([P, 2, P], F32, name="faded%d" % b) for b in range(BLOCKS)]
        faded_one = sb.tile([P, BLOCKS // 2, P], F32, name="faded_one")
        kept = []
        for c in range(CHUNKS):
            turned = bank(c % 2 if c > 0 else 4, [P, PER_CHUNK, 2, P], "turned%d" % c)
            for n in range(PER_CHUNK):
                b = c * PER_CHUNK + n
                for k in range(2):
                    nc.tensor.transpose(turned[:, n, k, :], old_high[:, k, b * P : (b + 1) * P], identity[:])
            for n in range(PER_CHUNK):
                b = c * PER_CHUNK + n
                nc.scalar.activation(faded[b][:], turned[:, n, :, :], ACT.Copy, scale=fade_cols[:, b : b + 1])
        turned_one = bank(0, [P, BLOCKS // 2, P], "turned_one")
        for n in range(BLOCKS // 2):
            b = BLOCKS // 2 + n
            nc.tensor.transpose(turned_one[:, n, :], old_low[:, 1, b * P : (b + 1) * P], identity[:])
        for n in range(BLOCKS // 2):
            b = BLOCKS // 2 + n
            nc.scalar.activation(faded_one[:, n, :], turned_one[:, n, :], ACT.Copy, scale=fade_cols[:, b : b + 1])
        for c in range(CHUNKS):
            back = bank(2 + c, [P, 2, CHUNK], "back%d" % c)
            for k in range(2):
                for n in range(PER_CHUNK):
                    nc.tensor.transpose(back[:, k, n * P : (n + 1) * P], faded[c * PER_CHUNK + n][:, k, :], identity[:])
            kept.append(back)
        kept_one = bank(6, [P, WIDE], "back_one")
        for n in range(BLOCKS // 2):
            nc.tensor.transpose(kept_one[:, n * P : (n + 1) * P], faded_one[:, n, :], identity[:])

        faded_low = sb.tile([P, U + WIDE], F32, name="faded_low", tag="rounded1", align_bytes=64)
        y = [sb.tile([P, PACK, WIDE], F32, name="y%d" % h) for h in range(2)]
        y_bytes = sb.tile([P, U], U8, name="y_bytes", align_bytes=64)
        words_out = out_1[0].rearrange("p c r -> p (c r)").bitcast(I32)
        y_bf = [sb.tile([P, CHUNK, PACK], BF16, name="y_bf%d" % c, align_bytes=64) for c in range(CHUNKS)]
        y_codes = [sb.tile([P, WIDE], U32, name="y_codes%d" % h, align_bytes=64) for h in range(2)]

        nc.gpsimd.tensor_tensor(faded_low[:, 0:U], old_low[:, 0, :], fade_all[:], ALU.mult)
        nc.gpsimd.tensor_tensor(faded_low[:, U : U + WIDE], old_low[:, 1, 0:WIDE], fade_all[:, 0:WIDE], ALU.mult)
        nc.gpsimd.tensor_tensor(y[0][:, 0, :], faded_low[:, 0:WIDE], placed[0][:, 0:WIDE], ALU.add)
        nc.scalar.dma_start(out_rows[:, 0, 0:WIDE], y[0][:, 0, :])
        nc.gpsimd.tensor_tensor(y[0][:, 1, :], faded_low[:, U : U + WIDE], placed[1][:, 0:WIDE], ALU.add)
        nc.scalar.dma_start(out_rows[:, 1, 0:WIDE], y[0][:, 1, :])
        nc.gpsimd.tensor_tensor(y[1][:, 0, :], faded_low[:, WIDE:U], placed[0][:, WIDE:U], ALU.add)
        nc.sync.dma_start(out_rows[:, 0, WIDE:U], y[1][:, 0, :])

        def add_high(c):
            h, n = divmod(c, 2)
            for k in range(2):
                nc.vector.tensor_tensor(
                    y[h][:, 2 + k, n * CHUNK : (n + 1) * CHUNK], kept[c][:, k, :], placed[2 + k][:, c * CHUNK : (c + 1) * CHUNK], ALU.add
                )
            nc.sync.dma_start(out_rows[:, 2:4, c * CHUNK : (c + 1) * CHUNK], y[h][:, 2:4, n * CHUNK : (n + 1) * CHUNK])

        def round_chunk(copy, c):
            h, n = divmod(c, 2)
            copy(
                y_bf[c][:].rearrange("p (a i) j -> p a j i", i=RUN),
                y[h][:, :, n * CHUNK : (n + 1) * CHUNK].rearrange("p j (a i) -> p a j i", i=RUN),
            )

        def quantise_chunk(c):
            h, n = divmod(c, 2)
            nc.vector.quantize_mx(
                y_codes[h][:, n * CHUNK : (n + 1) * CHUNK].bitcast(FP8X4),
                y_bytes[:, c * CHUNK : (c + 1) * CHUNK],
                y_bf[c][:].rearrange("p u j -> p (u j)"),
            )

        add_high(0)
        round_chunk(nc.scalar.copy, 0)
        add_high(1)
        round_chunk(nc.scalar.copy, 1)
        nc.vector.tensor_tensor(y[1][:, 1, :], kept_one[:], placed[1][:, WIDE:U], ALU.add)
        nc.sync.dma_start(out_rows[:, 1, WIDE:U], y[1][:, 1, :])
        add_high(2)
        round_chunk(nc.scalar.copy, 2)
        add_high(3)
        quantise_chunk(0)
        round_chunk(nc.vector.tensor_copy, 3)
        quantise_chunk(1)
        nc.sync.dma_start(words_out[:, 0:WIDE], y_codes[0][:].bitcast(I32))
        for n in range(2):
            c = 2 + n
            quantise_chunk(c)
            nc.sync.dma_start(words_out[:, c * CHUNK : (c + 1) * CHUNK], y_codes[1][:, n * CHUNK : (n + 1) * CHUNK].bitcast(I32))
        for quad in range(QUADS):
            (nc.scalar if quad < QUADS - 1 else nc.sync).dma_start(
                out_2[0, 4 * quad : 4 * quad + 4, :].bitcast(I32),
                y_bytes[32 * quad : 32 * quad + 4, :].bitcast(I32),
            )
